import numpy as np
import ml_dtypes


def mxq(x, axis, fmt="e4m3"):
    dtype, down = {"e4m3": (ml_dtypes.float8_e4m3fn, 7), "e5m2": (ml_dtypes.float8_e5m2, 14)}[fmt]
    v = np.moveaxis(np.asarray(x, np.float32).astype(ml_dtypes.bfloat16).astype(np.float64), axis, -1)
    blocks = v.reshape(v.shape[:-1] + (-1, 32))
    amax = np.abs(blocks).max(-1, keepdims=True)
    byte = np.maximum(np.where(amax > 0, np.frexp(amax)[1] - 1 + 127, 0) - down, 1)
    scale = np.exp2(byte - 127.0)
    codes = (blocks / scale).astype(np.float32).astype(dtype).astype(np.float64)
    return np.moveaxis((codes * scale).reshape(v.shape), -1, axis)


WIDE = False


def mx_kscale(k):
    if not WIDE:
        return np.ones(k)
    levels = np.array([10, -10, 5, -5, 0])
    if k % 512:
        return np.exp2(np.random.permutation(np.resize(levels, k // 32))).repeat(32)
    a = np.empty((k // 512, 16))
    for p in range(k // 512):
        a[p, :8] = np.random.permutation(np.resize(levels, 8))
        for g in range(8):
            far = levels[np.abs(levels - a[p, g]) >= 10]
            a[p, g + 8] = far[np.random.randint(len(far))]
    return np.exp2(a.ravel()).repeat(32)


def f64(x):
    return np.asarray(x).astype(np.float64)


def striped(idx):
    return np.tile(idx.reshape(-1, 16).T, (8, 1)).astype(np.uint16)


def unstriped(offs):
    return offs[:16].T.reshape(-1).astype(np.int64)


def striped8(idx):
    return np.concatenate([x.reshape(-1, 16).T for x in idx]).astype(np.uint16)


def runs(offs, k):
    lists = np.stack([offs[16 * r : 16 * r + 16].T.reshape(-1) for r in range(8)]).astype(np.int64)
    return lists[np.arange(k) % 512 // 64]


def pack_weight(w):
    k, n = w.shape
    w = f64(np.asarray(w, np.float32).astype(ml_dtypes.bfloat16)).reshape(k // 32, 32, n)
    amax = np.abs(w).max(1)
    byte = np.clip(np.where(amax > 0, np.frexp(amax)[1] - 1 + 127 - 7, 1), 1, 254)
    scaled = (w * np.exp2(127.0 - byte)[:, None, :]).reshape(k, n).astype(np.float32)
    words = np.ascontiguousarray(scaled.reshape(k // 512, 128, 4, n).transpose(0, 1, 3, 2)).astype(ml_dtypes.float8_e4m3fn).view(np.uint8)
    return words, np.ascontiguousarray(byte.astype(np.uint8).reshape(k // 512, 16, n))


def unpack_weight(words, scales):
    g, p, n, _ = words.shape
    vals = np.ascontiguousarray(words).view(ml_dtypes.float8_e4m3fn).astype(np.float64) * np.repeat(np.exp2(scales.astype(np.float64) - 127.0), 8, axis=1)[..., None]
    return vals.transpose(0, 1, 3, 2).reshape(g * 512, n)


E2M1 = np.array([0.0, 0.5, 1.0, 1.5, 2.0, 3.0, 4.0, 6.0, -0.0, -0.5, -1.0, -1.5, -2.0, -3.0, -4.0, -6.0])


def pack_fp4(w):
    k, n = w.shape
    w = f64(np.asarray(w, np.float32).astype(ml_dtypes.bfloat16)).reshape(k // 32, 32, n)
    amax = np.abs(w).max(1)
    mant, ex = np.frexp(amax / 6.0)
    byte = np.clip(np.where(amax > 0, np.where(mant > 0.5, ex, ex - 1) + 127, 1), 1, 254)
    scaled = (w * np.exp2(127.0 - byte)[:, None, :]).reshape(k, n).astype(np.float32)
    c = np.ascontiguousarray(scaled.reshape(k // 512, 128, 4, n).transpose(0, 1, 3, 2)).astype(ml_dtypes.float4_e2m1fn).view(np.uint8) & 0xF
    words = (c[..., 0::2] | (c[..., 1::2] << 4)).reshape(k // 512, 128, 2 * n)
    return np.ascontiguousarray(words), np.ascontiguousarray(byte.astype(np.uint8).reshape(k // 512, 16, n))


def unpack_fp4(words, scales):
    g, _, n = scales.shape
    words = np.ascontiguousarray(words).reshape(g, 128, n, 2)
    nib = np.empty((g, 128, n, 4), np.uint8)
    nib[..., 0::2] = words & 0xF
    nib[..., 1::2] = words >> 4
    vals = E2M1[nib] * np.repeat(np.exp2(scales.astype(np.float64) - 127.0), 8, axis=1)[..., None]
    return vals.transpose(0, 1, 3, 2).reshape(g * 512, n)


def relu(v):
    return np.maximum(v, 0.0)

def planes(y):
    n, m = y.shape
    v = y.astype(np.float32).astype(ml_dtypes.bfloat16).astype(np.float64).reshape(n // 32, 32, m)
    top = np.abs(v).max(1)
    byte = np.clip(np.where(top > 0, np.frexp(top)[1] - 1 + 127 - 7, 1), 1, 254)
    codes = (v * np.exp2(127.0 - byte)[:, None, :]).reshape(n, m).astype(np.float32).astype(ml_dtypes.float8_e4m3fn).view(np.uint8)
    words = codes.reshape(n // 512, 128, 4, m).transpose(0, 1, 3, 2)
    return np.ascontiguousarray(words), np.ascontiguousarray(byte.astype(np.uint8).reshape(n // 512, 16, m))


K, T, S, H, U, C, W = 512, 2048, 512, 512, 1024, 512, 4096


def setup_inputs():
    n = np.random.standard_normal
    s = mx_kscale(K)[:, None]
    packed_xT = pack_weight(n((K, T)) * s)
    packed_w1 = pack_fp4(n((K, H)) / np.sqrt(K) / s)
    return {
        "x_words": packed_xT[0],
        "x_scales": packed_xT[1],
        "w1_words": packed_w1[0],
        "w1_scales": packed_w1[1],
        "gs": (np.random.uniform(0.5, 1.5, (K, 1)) / s).astype(np.float32),
        "offs": striped8(np.random.randint(0, T, (8, S))),
        "n1": striped8(np.stack([np.random.permutation(U)[:S] for _ in range(8)])),
        "n2": striped8(np.stack([np.random.permutation(S) for _ in range(8)])),
        "cand": striped8(np.random.randint(0, T, (8, C))),
        "n3": striped(np.random.randint(0, U, W)),
    }


def reference(x_words, x_scales, w1_words, w1_scales, gs, offs, n1, n2, cand, n3):
    x_cand = unpack_weight(x_words, x_scales)[np.arange(K)[:, None], runs(cand, K)]
    xq = unpack_weight(x_words, x_scales)[np.arange(K)[:, None], runs(offs, K)]
    y = unpack_fp4(w1_words, w1_scales).T @ xq
    nw = y - (relu(y[np.arange(H)[:, None], runs(n2, H)]))
    pg = np.zeros((H, U))
    pg[np.arange(H)[:, None], runs(n1, H)] = nw
    z = f64(gs) * pg
    s = 0.0625 * ((x_cand.T @ mxq(z, 0, "e4m3")))
    mb = s[:, unstriped(n3)]
    mx = mb.reshape(C, U, 4).max(axis=2)
    mn = mb.reshape(C, U, 4).min(axis=2)
    out_0 = mx - (0.5 * mn)
    return (out_0,) + planes(out_0)

@@ -1,0 +1,204 @@
+from contextlib import ExitStack
+
+import concourse.mybir as mybir
+
+K, T, S, H, U, C, W = 512, 2048, 512, 512, 1024, 512, 4096
+FLOPS = 2 * K * H * S + 2 * K * C * U
+
+F32 = mybir.dt.float32
+BF16 = mybir.dt.bfloat16
+I32 = mybir.dt.int32
+U32 = mybir.dt.uint32
+U16 = mybir.dt.uint16
+U8 = mybir.dt.uint8
+FP8X4 = mybir.dt.float8_e4m3fn_x4
+FP4X4 = mybir.dt.float4_e2m1fn_x4
+ALU = mybir.AluOpType
+ACT = mybir.ActivationFunctionType
+
+P = 128
+PACK = 4
+HALF = 512
+BLOCK = 256
+SPARE = 16
+
+
+def scale_rows_into_place(queue, plane):
+    for r in range(1, PACK):
+        queue.dma_start(plane[r:P:32, :].bitcast(I32), plane[8 * r : P : 32, :].bitcast(I32))
+
+
+def tile_picked_hcandpagezgspan_none_po_kernel(tc, x_words, x_scales, w1_words, w1_scales, gs, offs, n1, n2, cand, n3, out_0, out_1, out_2):
+    nc = tc.nc
+    with ExitStack() as ctx:
+        lists = ctx.enter_context(tc.tile_pool(name="lists", bufs=1))
+        keep = ctx.enter_context(tc.tile_pool(name="keep", bufs=1))
+        ring = ctx.enter_context(tc.tile_pool(name="ring", bufs=2))
+        psum = ctx.enter_context(tc.psum_pool(name="psum", bufs=1))
+
+        offs_sb = lists.tile([P, S // 16], U16, name="offs_sb")
+        n2_sb = lists.tile([P, S // 16], U16, name="n2_sb")
+        n1_sb = lists.tile([P, S // 16], U16, name="n1_sb")
+        cand_sb = lists.tile([P, C // 16], U16, name="cand_sb")
+        n3_sb = lists.tile([P, W // 16], U16, name="n3_sb")
+
+        x_bytes = keep.tile([P, T], U8, name="x_bytes", align_bytes=64)
+        w_bytes = keep.tile([P, H], U8, name="w_bytes", align_bytes=64)
+        x_table = keep.tile([P, T], U32, name="x_table", align_bytes=64)
+        w_raw = keep.tile([P, 2 * H], U8, name="w_raw", align_bytes=64)
+        gs_sb = keep.tile([P, PACK], F32, name="gs_sb")
+
+        nc.vector.memset(x_bytes[:].bitcast(I32), 0)
+        nc.vector.memset(w_bytes[:].bitcast(I32), 0)
+        nc.sync.dma_start(offs_sb[:], offs)
+        nc.sync.dma_start(x_bytes[0:P:8, :].bitcast(I32), x_scales[0].bitcast(I32))
+        nc.sync.dma_start(w_bytes[0:P:8, :].bitcast(I32), w1_scales[0].bitcast(I32))
+        nc.scalar.dma_start(w_raw[:].bitcast(I32), w1_words[0].bitcast(I32))
+        nc.scalar.dma_start(x_table[:].bitcast(I32), x_words[0].rearrange("p n t -> p (n t)").bitcast(I32))
+        nc.sync.dma_start(cand_sb[:], cand)
+        nc.sync.dma_start(n2_sb[:], n2)
+        nc.sync.dma_start(n1_sb[:], n1)
+        nc.sync.dma_start(n3_sb[:], n3)
+        nc.gpsimd.dma_start(gs_sb[:], gs.rearrange("(p t) o -> p (t o)", t=PACK))
+
+        pages = [keep.tile([P, U], F32, name=f"page{t}") for t in range(PACK)]
+        relu_y = [keep.tile([P, 2 * S], F32, name=f"relu_y{t}") for t in range(PACK)]
+        scores = [keep.tile([P, U + SPARE], F32, name=f"scores{t}") for t in range(PACK)]
+        for t in range(PACK):
+            nc.gpsimd.memset(relu_y[t][:, S:], 0.0)
+        for t in range(PACK):
+            nc.vector.memset(pages[t][:], 0.0)
+        for t in range(PACK):
+            nc.gpsimd.memset(scores[t][:, U:], 0.0)
+
+        xq_picked = keep.tile([P, S], U8, name="xq_picked", align_bytes=64)
+        xq_scales = keep.tile([P, S], U8, name="xq_scales", align_bytes=64)
+        xq_words = keep.tile([P, S], U32, name="xq_words", align_bytes=64)
+        w_scales = keep.tile([P, H], U8, name="w_scales", align_bytes=64)
+        w_words = keep.tile([P, 2 * H], U8, name="w_words", align_bytes=64)
+        nc.vector.tensor_copy(xq_picked[:], x_bytes[:].indirect(offs_sb[:]))
+        nc.vector.tensor_copy(xq_scales[:].bitcast(I32), xq_picked[:].bitcast(I32))
+        scale_rows_into_place(nc.sync, xq_scales)
+        nc.vector.tensor_copy(
+            w_scales[:].rearrange("p (t m) -> p t m", t=PACK), w_bytes[:].rearrange("p (m t) -> p t m", t=PACK)
+        )
+        scale_rows_into_place(nc.scalar, w_scales)
+        nc.vector.tensor_copy(
+            w_words[:].rearrange("p (t m b) -> p t m b", t=PACK, b=2),
+            w_raw[:].rearrange("p (m t b) -> p t m b", t=PACK, b=2),
+        )
+        nc.vector.tensor_copy(xq_words[:], x_table[:].indirect(offs_sb[:]))
+
+        xc_picked = keep.tile([P, C], U8, name="xc_picked", align_bytes=64)
+        xc_scales = keep.tile([P, C], U8, name="xc_scales", align_bytes=64)
+        xc_gathered = keep.tile([P, C], U32, name="xc_gathered", align_bytes=64)
+        xc_words = keep.tile([P, C], U32, name="xc_words", align_bytes=64)
+        nc.vector.tensor_copy(xc_picked[:], x_bytes[:].indirect(cand_sb[:]))
+        nc.vector.tensor_copy(xc_gathered[:], x_table[:].indirect(cand_sb[:]))
+        nc.vector.tensor_copy(
+            xc_scales[:].rearrange("p (t m) -> p t m", t=PACK), xc_picked[:].rearrange("p (m t) -> p t m", t=PACK)
+        )
+        scale_rows_into_place(nc.sync, xc_scales)
+        nc.vector.tensor_copy(
+            xc_words[:].bitcast(I32).rearrange("p (t m) -> p t m", t=PACK),
+            xc_gathered[:].bitcast(I32).rearrange("p (m t) -> p t m", t=PACK),
+        )
+
+        z_planes = keep.tile([P, PACK, U], BF16, name="z_planes", align_bytes=64)
+        for t in range(PACK):
+            y_bank = psum.tile([P, S], F32, name=f"y_bank{t}", tag=f"bank{t}")
+            nc.tensor.matmul_mx(
+                out=y_bank[:],
+                lhsT=w_words[:, 2 * P * t : 2 * P * (t + 1)].bitcast(FP4X4),
+                lhsT_scale=w_scales[:, P * t : P * (t + 1)],
+                rhs=xq_words[:].bitcast(FP8X4),
+                rhs_scale=xq_scales[:],
+                start=True,
+                stop=True,
+            )
+            y_sb = keep.tile([P, S], F32, name=f"y_sb{t}")
+            pulled = keep.tile([P, S], F32, name=f"pulled{t}")
+            nc.scalar.activation(relu_y[t][:, :S], y_bank[:], ACT.Relu)
+            nc.scalar.activation(pulled[:], relu_y[t][:].indirect(n2_sb[:]), ACT.Copy, scale=-1.0)
+            nc.scalar.copy(y_sb[:], y_bank[:])
+            nc.vector.tensor_tensor(pages[t][:].indirect(n1_sb[:]), y_sb[:], pulled[:], ALU.add)
+        for t in range(PACK - 1):
+            nc.scalar.activation(z_planes[:, t, :], pages[t][:], ACT.Copy, scale=gs_sb[:, t : t + 1])
+
+        z_words = keep.tile([P, U], U32, name="z_words", align_bytes=64)
+        z_scales = keep.tile([P, U], U8, name="z_scales", align_bytes=64)
+        last = PACK - 1
+        halves = [slice(HALF * h, HALF * (h + 1)) for h in range(U // HALF)]
+        nc.vector.tensor_scalar(z_planes[:, last, halves[0]], pages[last][:, halves[0]], gs_sb[:, last:], None, ALU.mult)
+        nc.scalar.activation(z_planes[:, last, halves[1]], pages[last][:, halves[1]], ACT.Copy, scale=gs_sb[:, last:])
+        for h, cols in enumerate(halves):
+            z_woven = keep.tile([P, HALF, PACK], BF16, name=f"z_woven{h}", align_bytes=64)
+            nc.vector.tensor_copy(
+                z_woven[:].rearrange("p (c i) t -> p c t i", i=4),
+                z_planes[:, :, cols].rearrange("p t (c i) -> p c t i", i=4),
+            )
+            nc.vector.quantize_mx(
+                out=z_words[:, cols].bitcast(FP8X4),
+                scales=z_scales[:, cols],
+                in_=z_woven[:].rearrange("p w t -> p (w t)"),
+            )
+            for t in range(PACK):
+                s_bank = psum.tile([P, HALF], F32, name=f"s_bank{h}{t}", tag=f"bank{PACK * (1 - h) + t}")
+                nc.tensor.matmul_mx(
+                    out=s_bank[:],
+                    lhsT=xc_words[:, P * t : P * (t + 1)].bitcast(FP8X4),
+                    lhsT_scale=xc_scales[:, P * t : P * (t + 1)],
+                    rhs=z_words[:, cols].bitcast(FP8X4),
+                    rhs_scale=z_scales[:, cols],
+                    start=True,
+                    stop=True,
+                )
+                if h == 0 or t == 0:
+                    nc.scalar.activation(scores[t][:, cols], s_bank[:], ACT.Copy, scale=0.0625)
+                else:
+                    nc.vector.tensor_scalar(scores[t][:, cols], s_bank[:], 0.0625, None, ALU.mult)
+
+        out_rows = out_0.rearrange("(p t) w -> p t w", t=PACK)
+        out_words_dram = out_1[0].rearrange("p w t -> p (w t)").bitcast(I32)
+        o_words = keep.tile([P, U], U32, name="o_words", align_bytes=64)
+        o_scales = keep.tile([P, U], U8, name="o_scales", align_bytes=64)
+        for j in range(U // BLOCK):
+            cols = slice(BLOCK * j, BLOCK * (j + 1))
+            entries = n3_sb[:, BLOCK // 4 * j : BLOCK // 4 * (j + 1)]
+            result = keep.tile([P, PACK, BLOCK], F32, name=f"result{j}")
+            for pair in range(2):
+                members = ring.tile([P, 2, 4 * BLOCK], F32, name="members", bufs=3)
+                for i in range(2):
+                    t = 2 * pair + i
+                    if j == 0 and t == 1:
+                        nc.vector.tensor_copy(members[:, i, :], scores[t][:].indirect(entries))
+                    else:
+                        nc.scalar.activation(members[:, i, :], scores[t][:].indirect(entries), ACT.Copy)
+                four = members[:].rearrange("p i (w m) -> p (i w) m", m=4)
+                larger = ring.tile([P, 2 * BLOCK, 2], F32, name="larger")
+                smaller = ring.tile([P, 2 * BLOCK, 2], F32, name="smaller")
+                largest = ring.tile([P, 2 * BLOCK], F32, name="largest")
+                smallest = ring.tile([P, 2 * BLOCK], F32, name="smallest")
+                nc.vector.tensor_tensor(larger[:], four[:, :, 0:2], four[:, :, 2:4], ALU.max)
+                nc.vector.tensor_tensor(smaller[:], four[:, :, 0:2], four[:, :, 2:4], ALU.min)
+                nc.vector.tensor_tensor(largest[:], larger[:, :, 0], larger[:, :, 1], ALU.max)
+                nc.vector.tensor_tensor(smallest[:], smaller[:, :, 0], smaller[:, :, 1], ALU.min)
+                nc.vector.scalar_tensor_tensor(
+                    result[:, 2 * pair : 2 * pair + 2, :].rearrange("p i w -> p (i w)"),
+                    smallest[:], -0.5, largest[:], ALU.mult, ALU.add,
+                )
+            nc.sync.dma_start(out_rows[:, :, cols], result[:])
+            rounded = ring.tile([P, BLOCK, PACK], BF16, name="rounded", align_bytes=64)
+            nc.vector.tensor_copy(
+                rounded[:].rearrange("p (c i) t -> p c t i", i=4),
+                result[:].rearrange("p t (c i) -> p c t i", i=4),
+            )
+            nc.vector.quantize_mx(
+                out=o_words[:, cols].bitcast(FP8X4),
+                scales=o_scales[:, cols],
+                in_=rounded[:].rearrange("p w t -> p (w t)"),
+            )
+            nc.sync.dma_start(out_words_dram[:, cols], o_words[:, cols].bitcast(I32))
+        for q in range(4):
+            queue = nc.scalar if q % 2 else nc.sync
+            queue.dma_start(out_2[0, 4 * q : 4 * q + 4, :].bitcast(I32), o_scales[32 * q : 32 * q + 4, :].bitcast(I32))

@@ -19,7 +19,10 @@ ACT = mybir.ActivationFunctionType
 P = 128
 PACK = 4
 HALF = 512
-BLOCK = 256
+QUARTER = 256
+BLOCKS = [256, 256, 256, 128, 128]
+TILES = [2, 2, 2, 4, 2]
+ROUND_ON_SCALAR = (2, 3)
 SPARE = 16
 
 
@@ -42,38 +45,33 @@ def tile_picked_hcandpagezgspan_none_po_kernel(tc, x_words, x_scales, w1_words, 
         cand_sb = lists.tile([P, C // 16], U16, name="cand_sb")
         n3_sb = lists.tile([P, W // 16], U16, name="n3_sb")
 
-        x_bytes = keep.tile([P, T], U8, name="x_bytes", align_bytes=64)
+        x_bytes = keep.tile([P, T], U8, name="x_bytes", tag="x_bytes", align_bytes=64)
         w_bytes = keep.tile([P, H], U8, name="w_bytes", align_bytes=64)
-        x_table = keep.tile([P, T], U32, name="x_table", align_bytes=64)
-        w_raw = keep.tile([P, 2 * H], U8, name="w_raw", align_bytes=64)
+        x_table = keep.tile([P, T], U32, name="x_table", tag="page3", align_bytes=64)
+        w_raw = keep.tile([P, 2 * H], U8, name="w_raw", tag="page2", align_bytes=64)
         gs_sb = keep.tile([P, PACK], F32, name="gs_sb")
 
-        nc.vector.memset(x_bytes[:].bitcast(I32), 0)
-        nc.vector.memset(w_bytes[:].bitcast(I32), 0)
         nc.sync.dma_start(offs_sb[:], offs)
-        nc.sync.dma_start(x_bytes[0:P:8, :].bitcast(I32), x_scales[0].bitcast(I32))
-        nc.sync.dma_start(w_bytes[0:P:8, :].bitcast(I32), w1_scales[0].bitcast(I32))
+        nc.sync.dma_start(x_bytes[:].bitcast(I32), x_scales[0].bitcast(I32).unsqueeze(1).to_broadcast([16, 8, T // 4]))
+        nc.scalar.dma_start(w_bytes[:].bitcast(I32), w1_scales[0].bitcast(I32).unsqueeze(1).to_broadcast([16, 8, H // 4]))
         nc.scalar.dma_start(w_raw[:].bitcast(I32), w1_words[0].bitcast(I32))
-        nc.scalar.dma_start(x_table[:].bitcast(I32), x_words[0].rearrange("p n t -> p (n t)").bitcast(I32))
         nc.sync.dma_start(cand_sb[:], cand)
         nc.sync.dma_start(n2_sb[:], n2)
         nc.sync.dma_start(n1_sb[:], n1)
+        nc.sync.dma_start(x_table[:].bitcast(I32), x_words[0].rearrange("p n t -> p (n t)").bitcast(I32))
         nc.sync.dma_start(n3_sb[:], n3)
         nc.gpsimd.dma_start(gs_sb[:], gs.rearrange("(p t) o -> p (t o)", t=PACK))
 
-        pages = [keep.tile([P, U], F32, name=f"page{t}") for t in range(PACK)]
-        relu_y = [keep.tile([P, 2 * S], F32, name=f"relu_y{t}") for t in range(PACK)]
+        pages = [keep.tile([P, U], F32, name=f"page{t}") for t in range(2)]
+        relu_y = [keep.tile([P, S], F32, name=f"relu_y{t}") for t in range(PACK)]
         scores = [keep.tile([P, U + SPARE], F32, name=f"scores{t}") for t in range(PACK)]
-        for t in range(PACK):
-            nc.gpsimd.memset(relu_y[t][:, S:], 0.0)
-        for t in range(PACK):
+        for t in range(2):
             nc.vector.memset(pages[t][:], 0.0)
         for t in range(PACK):
             nc.gpsimd.memset(scores[t][:, U:], 0.0)
 
-        xq_picked = keep.tile([P, S], U8, name="xq_picked", align_bytes=64)
+        xq_picked = keep.tile([P, S], U8, name="xq_picked", tag="picked", align_bytes=64)
         xq_scales = keep.tile([P, S], U8, name="xq_scales", align_bytes=64)
-        xq_words = keep.tile([P, S], U32, name="xq_words", align_bytes=64)
         w_scales = keep.tile([P, H], U8, name="w_scales", align_bytes=64)
         w_words = keep.tile([P, 2 * H], U8, name="w_words", align_bytes=64)
         nc.vector.tensor_copy(xq_picked[:], x_bytes[:].indirect(offs_sb[:]))
@@ -87,118 +85,179 @@ def tile_picked_hcandpagezgspan_none_po_kernel(tc, x_words, x_scales, w1_words, 
             w_words[:].rearrange("p (t m b) -> p t m b", t=PACK, b=2),
             w_raw[:].rearrange("p (m t b) -> p t m b", t=PACK, b=2),
         )
+        xc_picked = keep.tile([P, C], U8, name="xc_picked", tag="picked", align_bytes=64)
+        nc.vector.tensor_copy(xc_picked[:], x_bytes[:].indirect(cand_sb[:]))
+        xq_words = keep.tile([P, S], U32, name="xq_words", tag="x_bytes", align_bytes=64)
         nc.vector.tensor_copy(xq_words[:], x_table[:].indirect(offs_sb[:]))
 
-        xc_picked = keep.tile([P, C], U8, name="xc_picked", align_bytes=64)
         xc_scales = keep.tile([P, C], U8, name="xc_scales", align_bytes=64)
         xc_gathered = keep.tile([P, C], U32, name="xc_gathered", align_bytes=64)
-        xc_words = keep.tile([P, C], U32, name="xc_words", align_bytes=64)
-        nc.vector.tensor_copy(xc_picked[:], x_bytes[:].indirect(cand_sb[:]))
         nc.vector.tensor_copy(xc_gathered[:], x_table[:].indirect(cand_sb[:]))
         nc.vector.tensor_copy(
             xc_scales[:].rearrange("p (t m) -> p t m", t=PACK), xc_picked[:].rearrange("p (m t) -> p t m", t=PACK)
         )
         scale_rows_into_place(nc.sync, xc_scales)
+        for t in range(2, PACK):
+            pages.append(keep.tile([P, U], F32, name=f"page{t}", tag=f"page{t}", align_bytes=64))
+            nc.gpsimd.memset(pages[t][:], 0.0)
+        z_pairs = [keep.tile([P, 2, QUARTER, 2], BF16, name=f"z_pairs{h}", align_bytes=64) for h in range(U // QUARTER)]
+        for t in range(PACK):
+            pieces = 2 if t == 0 else 1
+            n = S // pieces
+            y_sb = keep.tile([P, S], F32, name=f"y_sb{t}")
+            pulled = keep.tile([P, S], F32, name=f"pulled{t}", tag=f"pulled{t}", align_bytes=64)
+            banks = []
+            for e in range(pieces):
+                y_bank = psum.tile([P, n], F32, name=f"y_bank{t}{e}", tag=f"bank{PACK * e + t}")
+                banks.append(y_bank)
+                nc.tensor.matmul_mx(
+                    out=y_bank[:],
+                    lhsT=w_words[:, 2 * P * t : 2 * P * (t + 1)].bitcast(FP4X4),
+                    lhsT_scale=w_scales[:, P * t : P * (t + 1)],
+                    rhs=xq_words[:, n * e : n * (e + 1)].bitcast(FP8X4),
+                    rhs_scale=xq_scales[:, n * e : n * (e + 1)],
+                    start=True,
+                    stop=True,
+                )
+                nc.scalar.activation(relu_y[t][:, n * e : n * (e + 1)], y_bank[:], ACT.Relu)
+            for e in range(pieces):
+                if t == 0:
+                    nc.vector.tensor_copy(y_sb[:, n * e : n * (e + 1)], banks[e][:])
+                else:
+                    nc.scalar.copy(y_sb[:], banks[e][:])
+            for e in range(2):
+                nc.scalar.activation(
+                    pulled[:, S // 2 * e : S // 2 * (e + 1)],
+                    relu_y[t][:].indirect(n2_sb[:, S // 32 * e : S // 32 * (e + 1)]),
+                    ACT.Copy,
+                    scale=-1.0,
+                )
+            for e in range(pieces):
+                nc.vector.tensor_tensor(
+                    pages[t][:].indirect(n1_sb[:, n // 16 * e : n // 16 * (e + 1)]),
+                    y_sb[:, n * e : n * (e + 1)],
+                    pulled[:, n * e : n * (e + 1)],
+                    ALU.add,
+                )
+        xc_words = keep.tile([P, C], U32, name="xc_words", tag=f"pulled{PACK - 1}", align_bytes=64)
         nc.vector.tensor_copy(
             xc_words[:].bitcast(I32).rearrange("p (t m) -> p t m", t=PACK),
             xc_gathered[:].bitcast(I32).rearrange("p (m t) -> p t m", t=PACK),
         )
 
-        z_planes = keep.tile([P, PACK, U], BF16, name="z_planes", align_bytes=64)
+        quarters = [slice(QUARTER * h, QUARTER * (h + 1)) for h in range(U // QUARTER)]
         for t in range(PACK):
-            y_bank = psum.tile([P, S], F32, name=f"y_bank{t}", tag=f"bank{t}")
-            nc.tensor.matmul_mx(
-                out=y_bank[:],
-                lhsT=w_words[:, 2 * P * t : 2 * P * (t + 1)].bitcast(FP4X4),
-                lhsT_scale=w_scales[:, P * t : P * (t + 1)],
-                rhs=xq_words[:].bitcast(FP8X4),
-                rhs_scale=xq_scales[:],
-                start=True,
-                stop=True,
-            )
-            y_sb = keep.tile([P, S], F32, name=f"y_sb{t}")
-            pulled = keep.tile([P, S], F32, name=f"pulled{t}")
-            nc.scalar.activation(relu_y[t][:, :S], y_bank[:], ACT.Relu)
-            nc.scalar.activation(pulled[:], relu_y[t][:].indirect(n2_sb[:]), ACT.Copy, scale=-1.0)
-            nc.scalar.copy(y_sb[:], y_bank[:])
-            nc.vector.tensor_tensor(pages[t][:].indirect(n1_sb[:]), y_sb[:], pulled[:], ALU.add)
-        for t in range(PACK - 1):
-            nc.scalar.activation(z_planes[:, t, :], pages[t][:], ACT.Copy, scale=gs_sb[:, t : t + 1])
+            for h, cols in enumerate(quarters):
+                nc.scalar.activation(z_pairs[h][:, t // 2, :, t % 2], pages[t][:, cols], ACT.Copy, scale=gs_sb[:, t : t + 1])
 
         z_words = keep.tile([P, U], U32, name="z_words", align_bytes=64)
         z_scales = keep.tile([P, U], U8, name="z_scales", align_bytes=64)
-        last = PACK - 1
-        halves = [slice(HALF * h, HALF * (h + 1)) for h in range(U // HALF)]
-        nc.vector.tensor_scalar(z_planes[:, last, halves[0]], pages[last][:, halves[0]], gs_sb[:, last:], None, ALU.mult)
-        nc.scalar.activation(z_planes[:, last, halves[1]], pages[last][:, halves[1]], ACT.Copy, scale=gs_sb[:, last:])
-        for h, cols in enumerate(halves):
-            z_woven = keep.tile([P, HALF, PACK], BF16, name=f"z_woven{h}", align_bytes=64)
+
+        def score(t, cols, bank, on_scalar):
+            s_bank = psum.tile([P, cols.stop - cols.start], F32, name=f"s_bank{t}_{cols.start}", tag=f"bank{bank}")
+            nc.tensor.matmul_mx(
+                out=s_bank[:],
+                lhsT=xc_words[:, P * t : P * (t + 1)].bitcast(FP8X4),
+                lhsT_scale=xc_scales[:, P * t : P * (t + 1)],
+                rhs=z_words[:, cols].bitcast(FP8X4),
+                rhs_scale=z_scales[:, cols],
+                start=True,
+                stop=True,
+            )
+            if on_scalar:
+                nc.scalar.activation(scores[t][:, cols], s_bank[:], ACT.Copy, scale=0.0625)
+            else:
+                nc.vector.tensor_scalar(scores[t][:, cols], s_bank[:], 0.0625, None, ALU.mult)
+
+        woven = []
+        for h, cols in enumerate(quarters):
+            z_woven = keep.tile([P, QUARTER, PACK], BF16, name=f"z_woven{h}", align_bytes=64)
+            woven.append(z_woven)
             nc.vector.tensor_copy(
-                z_woven[:].rearrange("p (c i) t -> p c t i", i=4),
-                z_planes[:, :, cols].rearrange("p t (c i) -> p c t i", i=4),
+                z_woven[:].rearrange("p w t -> p (w t)").bitcast(I32).rearrange("p (w u) -> p w u", u=2),
+                z_pairs[h][:].rearrange("p u w e -> p (u w e)").bitcast(I32).rearrange("p (u w) -> p w u", u=2),
             )
-            nc.vector.quantize_mx(
-                out=z_words[:, cols].bitcast(FP8X4),
-                scales=z_scales[:, cols],
-                in_=z_woven[:].rearrange("p w t -> p (w t)"),
-            )
-            for t in range(PACK):
-                s_bank = psum.tile([P, HALF], F32, name=f"s_bank{h}{t}", tag=f"bank{PACK * (1 - h) + t}")
-                nc.tensor.matmul_mx(
-                    out=s_bank[:],
-                    lhsT=xc_words[:, P * t : P * (t + 1)].bitcast(FP8X4),
-                    lhsT_scale=xc_scales[:, P * t : P * (t + 1)],
-                    rhs=z_words[:, cols].bitcast(FP8X4),
-                    rhs_scale=z_scales[:, cols],
-                    start=True,
-                    stop=True,
+            for g in ([h - 1] if h else []) + ([h] if h == len(quarters) - 1 else []):
+                nc.vector.quantize_mx(
+                    out=z_words[:, quarters[g]].bitcast(FP8X4),
+                    scales=z_scales[:, quarters[g]],
+                    in_=woven[g][:].rearrange("p w t -> p (w t)"),
                 )
-                if h == 0 or t == 0:
-                    nc.scalar.activation(scores[t][:, cols], s_bank[:], ACT.Copy, scale=0.0625)
-                else:
-                    nc.vector.tensor_scalar(scores[t][:, cols], s_bank[:], 0.0625, None, ALU.mult)
+        for h, cols in enumerate(quarters):
+            for t in range(2):
+                score(t, cols, 2 * h + t, t == 0 or h < len(quarters) - 1)
+        for t in range(2, PACK):
+            for h in range(U // HALF):
+                score(t, slice(HALF * h, HALF * (h + 1)), 2 * (t - 2) + h, False)
 
         out_rows = out_0.rearrange("(p t) w -> p t w", t=PACK)
         out_words_dram = out_1[0].rearrange("p w t -> p (w t)").bitcast(I32)
         o_words = keep.tile([P, U], U32, name="o_words", align_bytes=64)
         o_scales = keep.tile([P, U], U8, name="o_scales", align_bytes=64)
-        for j in range(U // BLOCK):
-            cols = slice(BLOCK * j, BLOCK * (j + 1))
-            entries = n3_sb[:, BLOCK // 4 * j : BLOCK // 4 * (j + 1)]
-            result = keep.tile([P, PACK, BLOCK], F32, name=f"result{j}")
-            for pair in range(2):
-                members = ring.tile([P, 2, 4 * BLOCK], F32, name="members", bufs=3)
-                for i in range(2):
-                    t = 2 * pair + i
-                    if j == 0 and t == 1:
-                        nc.vector.tensor_copy(members[:, i, :], scores[t][:].indirect(entries))
-                    else:
-                        nc.scalar.activation(members[:, i, :], scores[t][:].indirect(entries), ACT.Copy)
-                four = members[:].rearrange("p i (w m) -> p (i w) m", m=4)
-                larger = ring.tile([P, 2 * BLOCK, 2], F32, name="larger")
-                smaller = ring.tile([P, 2 * BLOCK, 2], F32, name="smaller")
-                largest = ring.tile([P, 2 * BLOCK], F32, name="largest")
-                smallest = ring.tile([P, 2 * BLOCK], F32, name="smallest")
-                nc.vector.tensor_tensor(larger[:], four[:, :, 0:2], four[:, :, 2:4], ALU.max)
-                nc.vector.tensor_tensor(smaller[:], four[:, :, 0:2], four[:, :, 2:4], ALU.min)
-                nc.vector.tensor_tensor(largest[:], larger[:, :, 0], larger[:, :, 1], ALU.max)
-                nc.vector.tensor_tensor(smallest[:], smaller[:, :, 0], smaller[:, :, 1], ALU.min)
-                nc.vector.scalar_tensor_tensor(
-                    result[:, 2 * pair : 2 * pair + 2, :].rearrange("p i w -> p (i w)"),
-                    smallest[:], -0.5, largest[:], ALU.mult, ALU.add,
-                )
-            nc.sync.dma_start(out_rows[:, :, cols], result[:])
-            rounded = ring.tile([P, BLOCK, PACK], BF16, name="rounded", align_bytes=64)
-            nc.vector.tensor_copy(
-                rounded[:].rearrange("p (c i) t -> p c t i", i=4),
-                result[:].rearrange("p t (c i) -> p c t i", i=4),
+        starts = [sum(BLOCKS[:j]) for j in range(len(BLOCKS))]
+        results = [keep.tile([P, PACK, width], F32, name=f"result{j}") for j, width in enumerate(BLOCKS)]
+        units = [(j, t0, TILES[j]) for j in range(len(BLOCKS)) for t0 in range(0, PACK, TILES[j])]
+
+        def combine(j, t0, n, largest, smallest):
+            nc.vector.scalar_tensor_tensor(
+                results[j][:, t0 : t0 + n, :].rearrange("p i w -> p (i w)"), smallest[:], -0.5, largest[:], ALU.mult, ALU.add
             )
+
+        def round_block(j):
+            cols = slice(starts[j], starts[j] + BLOCKS[j])
+            nc.sync.dma_start(out_rows[:, :, cols], results[j][:])
+            rounded = keep.tile([P, BLOCKS[j], PACK], BF16, name=f"rounded{j}", align_bytes=64)
+            dst = rounded[:].rearrange("p (c i) t -> p c t i", i=4)
+            src = results[j][:].rearrange("p t (c i) -> p c t i", i=4)
+            if j in ROUND_ON_SCALAR:
+                nc.scalar.copy(dst, src)
+            else:
+                nc.vector.tensor_copy(dst, src)
+            return rounded
+
+        def quantize_block(j, rounded):
+            cols = slice(starts[j], starts[j] + BLOCKS[j])
             nc.vector.quantize_mx(
                 out=o_words[:, cols].bitcast(FP8X4),
                 scales=o_scales[:, cols],
                 in_=rounded[:].rearrange("p w t -> p (w t)"),
             )
             nc.sync.dma_start(out_words_dram[:, cols], o_words[:, cols].bitcast(I32))
+
+        before = None
+        waiting = []
+        for u, (j, t0, n) in enumerate(units):
+            width = BLOCKS[j]
+            entries = n3_sb[:, starts[j] // 4 : (starts[j] + width) // 4]
+            members = ring.tile([P, n, 4 * width], F32, name="members", bufs=3)
+            for i in range(n):
+                if u == 0 and i == 1:
+                    nc.vector.tensor_copy(members[:, i, :], scores[t0 + i][:].indirect(entries))
+                else:
+                    nc.scalar.activation(members[:, i, :], scores[t0 + i][:].indirect(entries), ACT.Copy)
+            four = members[:].rearrange("p i (w m) -> p (i w) m", m=4)
+            larger = ring.tile([P, n * width, 2], F32, name="larger")
+            smaller = ring.tile([P, n * width, 2], F32, name="smaller")
+            largest = ring.tile([P, n * width], F32, name="largest")
+            smallest = ring.tile([P, n * width], F32, name="smallest")
+            closes = before is not None and before[1] + before[2] == PACK
+            nc.vector.tensor_tensor(larger[:], four[:, :, 0:2], four[:, :, 2:4], ALU.max)
+            if before is not None:
+                combine(*before)
+            nc.vector.tensor_tensor(smaller[:], four[:, :, 0:2], four[:, :, 2:4], ALU.min)
+            if closes:
+                rounded = round_block(before[0])
+            nc.vector.tensor_tensor(largest[:], larger[:, :, 0], larger[:, :, 1], ALU.max)
+            nc.vector.tensor_tensor(smallest[:], smaller[:, :, 0], smaller[:, :, 1], ALU.min)
+            if closes and before[0] in ROUND_ON_SCALAR:
+                waiting.append((before[0], rounded))
+            elif closes:
+                quantize_block(before[0], rounded)
+            before = (j, t0, n, largest, smallest)
+        quantize_block(*waiting[0])
+        combine(*before)
+        quantize_block(*waiting[1])
+        quantize_block(before[0], round_block(before[0]))
         for q in range(4):
             queue = nc.scalar if q % 2 else nc.sync
             queue.dma_start(out_2[0, 4 * q : 4 * q + 4, :].bitcast(I32), o_scales[32 * q : 32 * q + 4, :].bitcast(I32))

@@ -47,8 +47,8 @@ def tile_picked_hcandpagezgspan_none_po_kernel(tc, x_words, x_scales, w1_words, 
 
         x_bytes = keep.tile([P, T], U8, name="x_bytes", tag="x_bytes", align_bytes=64)
         w_bytes = keep.tile([P, H], U8, name="w_bytes", align_bytes=64)
-        x_table = keep.tile([P, T], U32, name="x_table", tag="page3", align_bytes=64)
-        w_raw = keep.tile([P, 2 * H], U8, name="w_raw", tag="page2", align_bytes=64)
+        x_table = keep.tile([P, T], U32, name="x_table", tag="x_table", align_bytes=64)
+        w_raw = keep.tile([P, 2 * H], U8, name="w_raw", align_bytes=64)
         gs_sb = keep.tile([P, PACK], F32, name="gs_sb")
 
         nc.sync.dma_start(offs_sb[:], offs)
@@ -63,7 +63,7 @@ def tile_picked_hcandpagezgspan_none_po_kernel(tc, x_words, x_scales, w1_words, 
         nc.gpsimd.dma_start(gs_sb[:], gs.rearrange("(p t) o -> p (t o)", t=PACK))
 
         pages = [keep.tile([P, U], F32, name=f"page{t}") for t in range(2)]
-        relu_y = [keep.tile([P, S], F32, name=f"relu_y{t}") for t in range(PACK)]
+        relu_y = [keep.tile([P, S], F32, name=f"relu_y{t}", tag=f"relu_y{t}", align_bytes=64) for t in range(PACK)]
         scores = [keep.tile([P, U + SPARE], F32, name=f"scores{t}") for t in range(PACK)]
         for t in range(2):
             nc.vector.memset(pages[t][:], 0.0)
@@ -97,18 +97,18 @@ def tile_picked_hcandpagezgspan_none_po_kernel(tc, x_words, x_scales, w1_words, 
             xc_scales[:].rearrange("p (t m) -> p t m", t=PACK), xc_picked[:].rearrange("p (m t) -> p t m", t=PACK)
         )
         scale_rows_into_place(nc.sync, xc_scales)
-        for t in range(2, PACK):
-            pages.append(keep.tile([P, U], F32, name=f"page{t}", tag=f"page{t}", align_bytes=64))
-            nc.gpsimd.memset(pages[t][:], 0.0)
         z_pairs = [keep.tile([P, 2, QUARTER, 2], BF16, name=f"z_pairs{h}", align_bytes=64) for h in range(U // QUARTER)]
         for t in range(PACK):
+            if t >= 2:
+                pages.append(keep.tile([P, U], F32, name=f"page{t}", tag=("x_table", "relu_y0")[t - 2], align_bytes=64))
+                nc.gpsimd.memset(pages[t][:], 0.0)
             pieces = 2 if t == 0 else 1
             n = S // pieces
             y_sb = keep.tile([P, S], F32, name=f"y_sb{t}")
             pulled = keep.tile([P, S], F32, name=f"pulled{t}", tag=f"pulled{t}", align_bytes=64)
             banks = []
             for e in range(pieces):
-                y_bank = psum.tile([P, n], F32, name=f"y_bank{t}{e}", tag=f"bank{PACK * e + t}")
+                y_bank = psum.tile([P, n], F32, name=f"y_bank{t}{e}", tag=f"bank{(e + max(t - 1, 0)) % 2}")
                 banks.append(y_bank)
                 nc.tensor.matmul_mx(
                     out=y_bank[:],
@@ -188,7 +188,7 @@ def tile_picked_hcandpagezgspan_none_po_kernel(tc, x_words, x_scales, w1_words, 
                 score(t, cols, 2 * h + t, t == 0 or h < len(quarters) - 1)
         for t in range(2, PACK):
             for h in range(U // HALF):
-                score(t, slice(HALF * h, HALF * (h + 1)), 2 * (t - 2) + h, False)
+                score(t, slice(HALF * h, HALF * (h + 1)), 2 * t + h, False)
 
         out_rows = out_0.rearrange("(p t) w -> p t w", t=PACK)
         out_words_dram = out_1[0].rearrange("p w t -> p (w t)").bitcast(I32)

from contextlib import ExitStack

import concourse.mybir as mybir

K, T, S, H, U, C, W = 512, 2048, 512, 512, 1024, 512, 4096
FLOPS = 2 * K * H * S + 2 * K * C * U

F32 = mybir.dt.float32
BF16 = mybir.dt.bfloat16
I32 = mybir.dt.int32
U32 = mybir.dt.uint32
U16 = mybir.dt.uint16
U8 = mybir.dt.uint8
FP8X4 = mybir.dt.float8_e4m3fn_x4
FP4X4 = mybir.dt.float4_e2m1fn_x4
ALU = mybir.AluOpType
ACT = mybir.ActivationFunctionType

P = 128
PACK = 4
HALF = 512
QUARTER = 256
BLOCKS = [256, 256, 256, 128, 128]
TILES = [2, 2, 2, 4, 2]
ROUND_ON_SCALAR = (2, 3)
SPARE = 16


def scale_rows_into_place(queue, plane):
    for r in range(1, PACK):
        queue.dma_start(plane[r:P:32, :].bitcast(I32), plane[8 * r : P : 32, :].bitcast(I32))


def tile_picked_hcandpagezgspan_none_po_kernel(tc, x_words, x_scales, w1_words, w1_scales, gs, offs, n1, n2, cand, n3, out_0, out_1, out_2):
    nc = tc.nc
    with ExitStack() as ctx:
        lists = ctx.enter_context(tc.tile_pool(name="lists", bufs=1))
        keep = ctx.enter_context(tc.tile_pool(name="keep", bufs=1))
        ring = ctx.enter_context(tc.tile_pool(name="ring", bufs=2))
        psum = ctx.enter_context(tc.psum_pool(name="psum", bufs=1))

        offs_sb = lists.tile([P, S // 16], U16, name="offs_sb")
        n2_sb = lists.tile([P, S // 16], U16, name="n2_sb")
        n1_sb = lists.tile([P, S // 16], U16, name="n1_sb")
        cand_sb = lists.tile([P, C // 16], U16, name="cand_sb")
        n3_sb = lists.tile([P, W // 16], U16, name="n3_sb")

        x_bytes = keep.tile([P, T], U8, name="x_bytes", tag="x_bytes", align_bytes=64)
        w_bytes = keep.tile([P, H], U8, name="w_bytes", align_bytes=64)
        x_table = keep.tile([P, T], U32, name="x_table", tag="x_table", align_bytes=64)
        w_raw = keep.tile([P, 2 * H], U8, name="w_raw", align_bytes=64)
        gs_sb = keep.tile([P, PACK], F32, name="gs_sb")

        nc.sync.dma_start(offs_sb[:], offs)
        nc.sync.dma_start(x_bytes[:].bitcast(I32), x_scales[0].bitcast(I32).unsqueeze(1).to_broadcast([16, 8, T // 4]))
        nc.scalar.dma_start(w_bytes[:].bitcast(I32), w1_scales[0].bitcast(I32).unsqueeze(1).to_broadcast([16, 8, H // 4]))
        nc.scalar.dma_start(w_raw[:].bitcast(I32), w1_words[0].bitcast(I32))
        nc.sync.dma_start(cand_sb[:], cand)
        nc.sync.dma_start(n2_sb[:], n2)
        nc.sync.dma_start(n1_sb[:], n1)
        nc.sync.dma_start(x_table[:].bitcast(I32), x_words[0].rearrange("p n t -> p (n t)").bitcast(I32))
        nc.sync.dma_start(n3_sb[:], n3)
        nc.gpsimd.dma_start(gs_sb[:], gs.rearrange("(p t) o -> p (t o)", t=PACK))

        pages = [keep.tile([P, U], F32, name=f"page{t}") for t in range(2)]
        relu_y = [keep.tile([P, S], F32, name=f"relu_y{t}", tag=f"relu_y{t}", align_bytes=64) for t in range(PACK)]
        scores = [keep.tile([P, U + SPARE], F32, name=f"scores{t}") for t in range(PACK)]
        for t in range(2):
            nc.vector.memset(pages[t][:], 0.0)
        for t in range(PACK):
            nc.gpsimd.memset(scores[t][:, U:], 0.0)

        xq_picked = keep.tile([P, S], U8, name="xq_picked", tag="picked", align_bytes=64)
        xq_scales = keep.tile([P, S], U8, name="xq_scales", align_bytes=64)
        w_scales = keep.tile([P, H], U8, name="w_scales", align_bytes=64)
        w_words = keep.tile([P, 2 * H], U8, name="w_words", align_bytes=64)
        nc.vector.tensor_copy(xq_picked[:], x_bytes[:].indirect(offs_sb[:]))
        nc.vector.tensor_copy(xq_scales[:].bitcast(I32), xq_picked[:].bitcast(I32))
        scale_rows_into_place(nc.sync, xq_scales)
        nc.vector.tensor_copy(
            w_scales[:].rearrange("p (t m) -> p t m", t=PACK), w_bytes[:].rearrange("p (m t) -> p t m", t=PACK)
        )
        scale_rows_into_place(nc.scalar, w_scales)
        nc.vector.tensor_copy(
            w_words[:].rearrange("p (t m b) -> p t m b", t=PACK, b=2),
            w_raw[:].rearrange("p (m t b) -> p t m b", t=PACK, b=2),
        )
        xc_picked = keep.tile([P, C], U8, name="xc_picked", tag="picked", align_bytes=64)
        nc.vector.tensor_copy(xc_picked[:], x_bytes[:].indirect(cand_sb[:]))
        xq_words = keep.tile([P, S], U32, name="xq_words", tag="x_bytes", align_bytes=64)
        nc.vector.tensor_copy(xq_words[:], x_table[:].indirect(offs_sb[:]))

        xc_scales = keep.tile([P, C], U8, name="xc_scales", align_bytes=64)
        xc_gathered = keep.tile([P, C], U32, name="xc_gathered", align_bytes=64)
        nc.vector.tensor_copy(xc_gathered[:], x_table[:].indirect(cand_sb[:]))
        nc.vector.tensor_copy(
            xc_scales[:].rearrange("p (t m) -> p t m", t=PACK), xc_picked[:].rearrange("p (m t) -> p t m", t=PACK)
        )
        scale_rows_into_place(nc.sync, xc_scales)
        z_pairs = [keep.tile([P, 2, QUARTER, 2], BF16, name=f"z_pairs{h}", align_bytes=64) for h in range(U // QUARTER)]
        for t in range(PACK):
            if t >= 2:
                pages.append(keep.tile([P, U], F32, name=f"page{t}", tag=("x_table", "relu_y0")[t - 2], align_bytes=64))
                nc.gpsimd.memset(pages[t][:], 0.0)
            pieces = 2 if t == 0 else 1
            n = S // pieces
            y_sb = keep.tile([P, S], F32, name=f"y_sb{t}")
            pulled = keep.tile([P, S], F32, name=f"pulled{t}", tag=f"pulled{t}", align_bytes=64)
            banks = []
            for e in range(pieces):
                y_bank = psum.tile([P, n], F32, name=f"y_bank{t}{e}", tag=f"bank{(e + max(t - 1, 0)) % 2}")
                banks.append(y_bank)
                nc.tensor.matmul_mx(
                    out=y_bank[:],
                    lhsT=w_words[:, 2 * P * t : 2 * P * (t + 1)].bitcast(FP4X4),
                    lhsT_scale=w_scales[:, P * t : P * (t + 1)],
                    rhs=xq_words[:, n * e : n * (e + 1)].bitcast(FP8X4),
                    rhs_scale=xq_scales[:, n * e : n * (e + 1)],
                    start=True,
                    stop=True,
                )
                nc.scalar.activation(relu_y[t][:, n * e : n * (e + 1)], y_bank[:], ACT.Relu)
            for e in range(pieces):
                if t == 0:
                    nc.vector.tensor_copy(y_sb[:, n * e : n * (e + 1)], banks[e][:])
                else:
                    nc.scalar.copy(y_sb[:], banks[e][:])
            for e in range(2):
                nc.scalar.activation(
                    pulled[:, S // 2 * e : S // 2 * (e + 1)],
                    relu_y[t][:].indirect(n2_sb[:, S // 32 * e : S // 32 * (e + 1)]),
                    ACT.Copy,
                    scale=-1.0,
                )
            for e in range(pieces):
                nc.vector.tensor_tensor(
                    pages[t][:].indirect(n1_sb[:, n // 16 * e : n // 16 * (e + 1)]),
                    y_sb[:, n * e : n * (e + 1)],
                    pulled[:, n * e : n * (e + 1)],
                    ALU.add,
                )
        xc_words = keep.tile([P, C], U32, name="xc_words", tag=f"pulled{PACK - 1}", align_bytes=64)
        nc.vector.tensor_copy(
            xc_words[:].bitcast(I32).rearrange("p (t m) -> p t m", t=PACK),
            xc_gathered[:].bitcast(I32).rearrange("p (m t) -> p t m", t=PACK),
        )

        quarters = [slice(QUARTER * h, QUARTER * (h + 1)) for h in range(U // QUARTER)]
        for t in range(PACK):
            for h, cols in enumerate(quarters):
                nc.scalar.activation(z_pairs[h][:, t // 2, :, t % 2], pages[t][:, cols], ACT.Copy, scale=gs_sb[:, t : t + 1])

        z_words = keep.tile([P, U], U32, name="z_words", align_bytes=64)
        z_scales = keep.tile([P, U], U8, name="z_scales", align_bytes=64)

        def score(t, cols, bank, on_scalar):
            s_bank = psum.tile([P, cols.stop - cols.start], F32, name=f"s_bank{t}_{cols.start}", tag=f"bank{bank}")
            nc.tensor.matmul_mx(
                out=s_bank[:],
                lhsT=xc_words[:, P * t : P * (t + 1)].bitcast(FP8X4),
                lhsT_scale=xc_scales[:, P * t : P * (t + 1)],
                rhs=z_words[:, cols].bitcast(FP8X4),
                rhs_scale=z_scales[:, cols],
                start=True,
                stop=True,
            )
            if on_scalar:
                nc.scalar.activation(scores[t][:, cols], s_bank[:], ACT.Copy, scale=0.0625)
            else:
                nc.vector.tensor_scalar(scores[t][:, cols], s_bank[:], 0.0625, None, ALU.mult)

        woven = []
        for h, cols in enumerate(quarters):
            z_woven = keep.tile([P, QUARTER, PACK], BF16, name=f"z_woven{h}", align_bytes=64)
            woven.append(z_woven)
            nc.vector.tensor_copy(
                z_woven[:].rearrange("p w t -> p (w t)").bitcast(I32).rearrange("p (w u) -> p w u", u=2),
                z_pairs[h][:].rearrange("p u w e -> p (u w e)").bitcast(I32).rearrange("p (u w) -> p w u", u=2),
            )
            for g in ([h - 1] if h else []) + ([h] if h == len(quarters) - 1 else []):
                nc.vector.quantize_mx(
                    out=z_words[:, quarters[g]].bitcast(FP8X4),
                    scales=z_scales[:, quarters[g]],
                    in_=woven[g][:].rearrange("p w t -> p (w t)"),
                )
        for h, cols in enumerate(quarters):
            for t in range(2):
                score(t, cols, 2 * h + t, t == 0 or h < len(quarters) - 1)
        for t in range(2, PACK):
            for h in range(U // HALF):
                score(t, slice(HALF * h, HALF * (h + 1)), 2 * t + h, False)

        out_rows = out_0.rearrange("(p t) w -> p t w", t=PACK)
        out_words_dram = out_1[0].rearrange("p w t -> p (w t)").bitcast(I32)
        o_words = keep.tile([P, U], U32, name="o_words", align_bytes=64)
        o_scales = keep.tile([P, U], U8, name="o_scales", align_bytes=64)
        starts = [sum(BLOCKS[:j]) for j in range(len(BLOCKS))]
        results = [keep.tile([P, PACK, width], F32, name=f"result{j}") for j, width in enumerate(BLOCKS)]
        units = [(j, t0, TILES[j]) for j in range(len(BLOCKS)) for t0 in range(0, PACK, TILES[j])]

        def combine(j, t0, n, largest, smallest):
            nc.vector.scalar_tensor_tensor(
                results[j][:, t0 : t0 + n, :].rearrange("p i w -> p (i w)"), smallest[:], -0.5, largest[:], ALU.mult, ALU.add
            )

        def round_block(j):
            cols = slice(starts[j], starts[j] + BLOCKS[j])
            nc.sync.dma_start(out_rows[:, :, cols], results[j][:])
            rounded = keep.tile([P, BLOCKS[j], PACK], BF16, name=f"rounded{j}", align_bytes=64)
            dst = rounded[:].rearrange("p (c i) t -> p c t i", i=4)
            src = results[j][:].rearrange("p t (c i) -> p c t i", i=4)
            if j in ROUND_ON_SCALAR:
                nc.scalar.copy(dst, src)
            else:
                nc.vector.tensor_copy(dst, src)
            return rounded

        def quantize_block(j, rounded):
            cols = slice(starts[j], starts[j] + BLOCKS[j])
            nc.vector.quantize_mx(
                out=o_words[:, cols].bitcast(FP8X4),
                scales=o_scales[:, cols],
                in_=rounded[:].rearrange("p w t -> p (w t)"),
            )
            nc.sync.dma_start(out_words_dram[:, cols], o_words[:, cols].bitcast(I32))

        before = None
        waiting = []
        for u, (j, t0, n) in enumerate(units):
            width = BLOCKS[j]
            entries = n3_sb[:, starts[j] // 4 : (starts[j] + width) // 4]
            members = ring.tile([P, n, 4 * width], F32, name="members", bufs=3)
            for i in range(n):
                if u == 0 and i == 1:
                    nc.vector.tensor_copy(members[:, i, :], scores[t0 + i][:].indirect(entries))
                else:
                    nc.scalar.activation(members[:, i, :], scores[t0 + i][:].indirect(entries), ACT.Copy)
            four = members[:].rearrange("p i (w m) -> p (i w) m", m=4)
            larger = ring.tile([P, n * width, 2], F32, name="larger")
            smaller = ring.tile([P, n * width, 2], F32, name="smaller")
            largest = ring.tile([P, n * width], F32, name="largest")
            smallest = ring.tile([P, n * width], F32, name="smallest")
            closes = before is not None and before[1] + before[2] == PACK
            nc.vector.tensor_tensor(larger[:], four[:, :, 0:2], four[:, :, 2:4], ALU.max)
            if before is not None:
                combine(*before)
            nc.vector.tensor_tensor(smaller[:], four[:, :, 0:2], four[:, :, 2:4], ALU.min)
            if closes:
                rounded = round_block(before[0])
            nc.vector.tensor_tensor(largest[:], larger[:, :, 0], larger[:, :, 1], ALU.max)
            nc.vector.tensor_tensor(smallest[:], smaller[:, :, 0], smaller[:, :, 1], ALU.min)
            if closes and before[0] in ROUND_ON_SCALAR:
                waiting.append((before[0], rounded))
            elif closes:
                quantize_block(before[0], rounded)
            before = (j, t0, n, largest, smallest)
        quantize_block(*waiting[0])
        combine(*before)
        quantize_block(*waiting[1])
        quantize_block(before[0], round_block(before[0]))
        for q in range(4):
            queue = nc.scalar if q % 2 else nc.sync
            queue.dma_start(out_2[0, 4 * q : 4 * q + 4, :].bitcast(I32), o_scales[32 * q : 32 * q + 4, :].bitcast(I32))
